import numpy as np, ml_dtypes
CORES = [242,247,114,119]
N = 4
KB, QP, ROOT = 2, 256, 2
def setup_inputs(rng):
    return {"q": rng.standard_normal((N, 128, QP), dtype=np.float32).astype(ml_dtypes.bfloat16), "k": rng.standard_normal((N, 128, KB * 128), dtype=np.float32).astype(ml_dtypes.bfloat16), "v": rng.standard_normal((N, 128, KB * 128), dtype=np.float32).astype(ml_dtypes.bfloat16)}
def setup_inputs_big(rng):
    d = setup_inputs(rng)
    for k in ("q", "k", "v"): d[k] = (d[k].astype(np.float32) * 1024.0).astype(d[k].dtype)
    return d
def setup_inputs_small(rng):
    d = setup_inputs(rng)
    for k in ("q", "k", "v"): d[k] = (d[k].astype(np.float32) * (1 / 1024.0)).astype(d[k].dtype)
    return d
def setup_inputs_apart(rng):
    d = setup_inputs(rng)
    f = (10.0 ** rng.permutation(np.linspace(-1.5, 1.5, N))).astype(np.float32).reshape(N, 1, 1)
    for k in ("q", "k", "v"): d[k] = (d[k].astype(np.float32) * f).astype(d[k].dtype)
    return d
def reference(q, k, v):
    Q, K, V = q.astype(np.float64), k.astype(np.float64), v.astype(np.float64)
    o = np.zeros((128, QP))
    for j in range(N):
        for b in range(KB):
            o += V[j][:, 128 * b:128 * b + 128].T @ np.maximum(K[j][:, 128 * b:128 * b + 128].T @ Q[ROOT], 0.0)
    y = np.full((N, 128, QP), np.nan)
    y[ROOT] = o
    return {"y": y.astype(ml_dtypes.bfloat16 if q.dtype != np.float64 else np.float64)}

from concourse.mybir import AluOpType

NB, P, QP = 2, 128, 256
KW = NB * P
SW = NB * QP
NR = 4
NENG = 8

SCRATCH = {
    "kd": ("dram", [P, KW], "bfloat16"),
    "vd": ("dram", [P, KW], "bfloat16"),
    "qq": ("sbuf", [P, QP], "bfloat16"),
    "kk": ("sbuf", [P, NR * KW], "bfloat16"),
    "vv": ("sbuf", [P, NR * KW], "bfloat16"),
    "ss": ("sbuf", [P, NR * SW], "bfloat16"),
    "zz": ("sbuf", [P, SW], "float32"),
    "yo": ("sbuf", [P, QP], "bfloat16"),
    "ps0": ("psum", [P, SW], "float32"),
    "ps1": ("psum", [P, SW], "float32"),
    "ps2": ("psum", [P, SW], "float32"),
    "ps3": ("psum", [P, SW], "float32"),
    "po": ("psum", [P, SW], "float32"),
}
SEMAPHORES = (["ldq", "ldk", "ldv", "sent", "zero", "osum", "round", "stored"]
              + ["ak%d" % r for r in range(NR)] + ["av%d" % r for r in range(NR)]
              + ["sm%d" % r for r in range(NR)] + ["sr%d" % r for r in range(NR)])


def _engines(mask, n):
    out, bit, left = 0, 1, n
    while left and bit <= mask:
        if mask & bit:
            out |= bit
            left -= 1
        bit <<= 1
    return out


def _count(mask):
    return bin(mask).count("1")


def _sender(g, core, T, topo, rank, root_core):
    S = T.sem
    g.sync.dma_start(T.kd[:], T.k[:]).then_inc(S.ldk, 16)
    g.scalar.dma_start(T.vd[:], T.v[:]).then_inc(S.ldv, 16)
    rid, pid = topo.addr(root_core, core)
    m = _engines(topo.mask(core, root_core), NENG)
    lo, hi = rank * KW, (rank + 1) * KW
    g.wait_ge(S.ldk, 16)
    g.remote_dma(out_ap=T.kk[:, lo:hi], in_ap=T.kd[:], remote_sem=S["ak%d" % rank], local_sem=S.sent,
                 pid=pid, routing_id=rid, dma_engine_mask=m)
    g.wait_ge(S.ldv, 16)
    g.remote_dma(out_ap=T.vv[:, lo:hi], in_ap=T.vd[:], remote_sem=S["av%d" % rank], local_sem=S.sent,
                 pid=pid, routing_id=rid, dma_engine_mask=m)
    g.wait_ge(S.sent, 2 * _count(m))


def _root(g, core, T, topo, rank):
    S = T.sem
    te, ve = g.tensor, g.vector
    own = rank

    def far(r):
        c = T.cores[r]
        return 0 if (topo.host(c), topo.chip(c)) == (topo.host(core), topo.chip(core)) else 1

    others = sorted([r for r in range(NR) if r != own], key=lambda r: (far(r), r))
    landed = {r: _count(_engines(topo.mask(T.cores[r], core), NENG)) for r in others}

    g.sync.dma_start(T.qq[:], T.q[:]).then_inc(S.ldq, 16)
    g.scalar.dma_start(T.kk[:, own * KW:(own + 1) * KW], T.k[:]).then_inc(S.ldk, 16)
    g.sync.dma_start(T.vv[:, own * KW:(own + 1) * KW], T.v[:]).then_inc(S.ldv, 16)

    def s_mm(r):
        for b in range(NB):
            te.matmul(T["ps%d" % r][:, b * QP:(b + 1) * QP], T.kk[:, r * KW + b * P:r * KW + (b + 1) * P], T.qq[:],
                      True, True).then_inc(S["sm%d" % r], 1)

    n_o = [0]

    def o_mm(r):
        te.wait_ge(S["sr%d" % r], 1)
        for b in range(NB):
            n_o[0] += 1
            te.matmul(T.po[:, 0:QP], T.vv[:, r * KW + b * P:r * KW + (b + 1) * P],
                      T.ss[:, r * SW + b * QP:r * SW + (b + 1) * QP],
                      n_o[0] == 1, n_o[0] == NR * NB).then_inc(S.osum, 1)

    te.wait_ge(S.ldq, 16)
    te.wait_ge(S.ldk, 16)
    s_mm(own)
    te.wait_ge(S.ldv, 16)
    o_mm(own)
    for r in others:
        te.wait_ge(S["ak%d" % r], landed[r])
        s_mm(r)
    for r in others:
        te.wait_ge(S["av%d" % r], landed[r])
        o_mm(r)

    ve.memset(T.zz[:], 0.0).then_inc(S.zero, 1)
    ve.wait_ge(S.zero, 1)
    for r in [own] + others:
        ve.wait_ge(S["sm%d" % r], NB)
        ve.tensor_tensor(T.ss[:, r * SW:(r + 1) * SW], T["ps%d" % r][:], T.zz[:], AluOpType.max).then_inc(S["sr%d" % r], 1)
    ve.wait_ge(S.osum, NR * NB)
    ve.tensor_copy(T.yo[:], T.po[:, 0:QP]).then_inc(S.round, 1)

    g.sync.wait_ge(S.round, 1)
    g.sync.dma_start(T.y[:], T.yo[:]).then_inc(S.stored, 16)
    g.sync.wait_ge(S.stored, 16)


def rank_program(g, core, T, topo):
    rank = T.rank_of(core)
    if rank is None:
        return
    if rank == T.root:
        _root(g, core, T, topo, rank)
    else:
        _sender(g, core, T, topo, rank, T.cores[T.root])
